import numpy as np
import ml_dtypes


def mxq(x, axis, fmt="e4m3"):
    dtype, down = {"e4m3": (ml_dtypes.float8_e4m3fn, 7), "e5m2": (ml_dtypes.float8_e5m2, 14)}[fmt]
    v = np.moveaxis(np.asarray(x, np.float32).astype(ml_dtypes.bfloat16).astype(np.float64), axis, -1)
    blocks = v.reshape(v.shape[:-1] + (-1, 32))
    amax = np.abs(blocks).max(-1, keepdims=True)
    byte = np.maximum(np.where(amax > 0, np.frexp(amax)[1] - 1 + 127, 0) - down, 1)
    scale = np.exp2(byte - 127.0)
    codes = (blocks / scale).astype(np.float32).astype(dtype).astype(np.float64)
    return np.moveaxis((codes * scale).reshape(v.shape), -1, axis)


WIDE = False


def mx_kscale(k):
    if not WIDE:
        return np.ones(k)
    levels = np.array([30, -30])
    if k % 512:
        return np.exp2(np.random.permutation(np.resize(levels, k // 32))).repeat(32)
    a = np.empty((k // 512, 16))
    for p in range(k // 512):
        a[p, :8] = np.random.permutation(np.resize(levels, 8))
        for g in range(8):
            far = levels[np.abs(levels - a[p, g]) >= 10]
            a[p, g + 8] = far[np.random.randint(len(far))]
    return np.exp2(a.ravel()).repeat(32)


BF16 = ml_dtypes.bfloat16


def bf(x):
    return np.asarray(x, np.float32).astype(BF16)


def f64(x):
    return np.asarray(x).astype(np.float64)


E2M1 = np.array([0.0, 0.5, 1.0, 1.5, 2.0, 3.0, 4.0, 6.0, -0.0, -0.5, -1.0, -1.5, -2.0, -3.0, -4.0, -6.0])


def pack_weight(w, fmt):
    k, n = w.shape
    w = f64(bf(w)).reshape(k // 32, 32, n)
    amax = np.abs(w).max(1)
    if fmt in ("e4m3", "e5m2"):
        byte = np.frexp(amax)[1] - 1 + 127 - (7 if fmt == "e4m3" else 14)
    else:
        mant, ex = np.frexp(amax / 6.0)
        byte = np.where(mant > 0.5, ex, ex - 1) + 127
    byte = np.clip(np.where(amax > 0, byte, 1), 1, 254)
    scaled = (w * np.exp2(127.0 - byte)[:, None, :]).reshape(k, n).astype(np.float32)
    by_word = np.ascontiguousarray(scaled.reshape(k // 512, 128, 4, n).transpose(0, 1, 3, 2))
    if fmt in ("e4m3", "e5m2"):
        words = by_word.astype(ml_dtypes.float8_e4m3fn if fmt == "e4m3" else ml_dtypes.float8_e5m2).view(np.uint8)
    else:
        c = by_word.astype(ml_dtypes.float4_e2m1fn).view(np.uint8) & 0xF
        words = c[..., 0::2] | (c[..., 1::2] << 4)
    return np.ascontiguousarray(words), np.ascontiguousarray(byte.astype(np.uint8).reshape(k // 512, 16, n))


def unpack_weight(words, scales, fmt):
    g, p, n, _ = words.shape
    if fmt in ("e4m3", "e5m2"):
        vals = np.ascontiguousarray(words).view(ml_dtypes.float8_e4m3fn if fmt == "e4m3" else ml_dtypes.float8_e5m2).astype(np.float64)
    else:
        nib = np.empty((g, p, n, 4), np.uint8)
        nib[..., 0::2] = words & 0xF
        nib[..., 1::2] = words >> 4
        vals = E2M1[nib]
    vals = vals * np.repeat(np.exp2(scales.astype(np.float64) - 127.0), 8, axis=1)[..., None]
    return vals.transpose(0, 1, 3, 2).reshape(g * 512, n)


P, Q, N = 1024, 1536, 1536

SHIFT = 2.25
DF = 5.0


def setup_inputs():
    s = mx_kscale(P)
    t = mx_kscale(Q)
    z = np.random.standard_normal((P + Q, P + Q))
    v = (z + z.T) / np.sqrt(2.0 * (P + Q)) + SHIFT * np.eye(P + Q)
    G = np.random.standard_t(DF, (P, N)) * np.sqrt((DF - 2.0) / DF) * s[:, None]
    G_words, G_scales = pack_weight(G, "e5m2")
    return {"g_words": G_words,
            "g_scales": G_scales,
            "v_tt": bf(v[:P, :P] / s[:, None]),
            "score_eta": bf(np.random.standard_normal((N, Q)) * t),
            "v_et": bf(v[P:, :P] / t[:, None]),
            "obs_weight": bf(np.random.uniform(0.5, 1.5, N)),
            "theta": bf(np.random.standard_normal(P))}


def reference(g_words, g_scales, v_tt, score_eta, v_et, obs_weight, theta):
    G = unpack_weight(g_words, g_scales, "e5m2")
    own = G.T @ mxq(f64(v_tt), 0, "e4m3")
    nuis = mxq(f64(score_eta), 1, "e4m3") @ mxq(f64(v_et), 0, "e4m3")
    influence = (own + nuis) * f64(obs_weight)[:, None]
    return influence + f64(theta)[None, :]

@@ -1,0 +1,317 @@
+from contextlib import ExitStack
+
+import concourse.mybir as mybir
+from concourse.masks import make_identity
+
+FLOPS = 2 * 1536 * 1024 * (1024 + 1536)
+
+F32 = mybir.dt.float32
+BF16 = mybir.dt.bfloat16
+I32 = mybir.dt.int32
+U32 = mybir.dt.uint32
+U8 = mybir.dt.uint8
+E4M3 = mybir.dt.float8_e4m3fn_x4
+E5M2 = mybir.dt.float8_e5m2_x4
+MULT = mybir.AluOpType.mult
+ADD = mybir.AluOpType.add
+
+P = 128
+N = 1536
+PAR = 1024
+NT = 512
+S_COLS = 256
+VPATH = []
+SORD = 6
+
+
+def tile_score_influence_pseudovalues_e4_kernel(
+    tc, g_words, g_scales, v_tt, score_eta, v_et, obs_weight, theta, out
+):
+    nc = tc.nc
+    with ExitStack() as ctx:
+        keep = ctx.enter_context(tc.tile_pool(name="keep", bufs=1))
+        stage = ctx.enter_context(tc.tile_pool(name="stage", bufs=1))
+        psum = ctx.enter_context(tc.psum_pool(name="psum", bufs=1))
+        ctx.enter_context(tc.manual_schedule(engines={mybir.EngineType.PE, mybir.EngineType.SP}))
+
+        free = list(range(8))
+
+        def take():
+            b = free.pop(0)
+            return b, psum.tile([P, NT], F32, name="bank%d" % b, tag="bank%d" % b, bufs=1)
+
+        small = keep.tile([P, P], BF16, name="small")
+        small_f = keep.tile([P, P], F32, name="small_f")
+        cols = keep.tile([P, 20], F32, name="cols")
+        theta_b = keep.tile([P, PAR], F32, name="theta_b")
+        ident = keep.tile([P, P], F32, name="ident")
+        g_codes = keep.tile([P, 2, N], U32, name="g_codes", align_bytes=64)
+        g_plane = keep.tile([P, 2, N], U8, name="g_plane", align_bytes=64)
+
+
+        make_identity(nc, ident[:])
+        nc.vector.memset(small[:], 0.0)
+        nc.vector.memset(g_plane[:].rearrange("p g n -> p (g n)").bitcast(I32), 0)
+        w_rows = obs_weight.rearrange("(j p) -> j p", p=P)
+        def load_planes():
+            nc.sync.dma_start(out=small[0:8, :], in_=w_rows[0:8, :])
+            nc.sync.dma_start(out=small[8:12, :], in_=w_rows[8:12, :])
+            nc.sync.dma_start(out=small[12:20, :], in_=theta.rearrange("(j p) -> j p", p=P))
+            for q in range(4):
+                nc.sync.dma_start(
+                out=g_plane[32 * q : 32 * q + 4, :, :].rearrange("p g n -> p (g n)").bitcast(I32).rearrange("p (g n) -> p g n", g=2),
+                in_=g_scales[:, 4 * q : 4 * q + 4, :].bitcast(I32).rearrange("g r n -> r g n"),
+                )
+        s_raw = {}
+        w_raw = {}
+
+        def L_s(j, a=None):
+            if j not in s_raw:
+                t = keep.tile([P, 2, N], BF16, name="sraw%d" % j, align_bytes=64)
+                s_raw[j] = t
+            t = s_raw[j]
+            rows = score_eta[256 * j : 256 * j + 256, :].rearrange("(a p) k -> p a k", p=P)
+            if j in VPATH:
+                x = t[:].rearrange("p a k -> p (a k)").rearrange("p (b k) -> p b k", b=8)
+                rows = score_eta[256 * j : 256 * j + 256, :].rearrange("(b r) k -> r b k", r=32)
+                for q in range(4):
+                    nc.sync.dma_start(out=x[32 * q : 32 * q + 32, :, :], in_=rows[:, :, 384 * q : 384 * q + 384])
+            elif a is None:
+                nc.sync.dma_start(out=t[:], in_=rows)
+            else:
+                nc.sync.dma_start(out=t[:, a, :], in_=rows[:, a, :])
+
+        def L_w(c, h, lo=0, hi=NT):
+            if (c, h) not in w_raw:
+                w_raw[c, h] = keep.tile([P, 4, NT], BF16, name="wraw%d_%d" % (c, h), align_bytes=64)
+            t = w_raw[c, h]
+            wc = slice(NT * h + lo, NT * h + hi)
+            if c < 2:
+                nc.sync.dma_start(out=t[:, :, lo:hi], in_=v_tt[512 * c : 512 * c + 512, wc].rearrange("(p j) w -> p j w", j=4))
+            else:
+                nc.sync.dma_start(out=t[:, :, lo:hi], in_=v_et[512 * (c - 2) : 512 * (c - 1), wc].rearrange("(p j) w -> p j w", j=4))
+
+        def L_g(g, lo, hi):
+            nc.sync.dma_start(out=g_codes[:, g, lo:hi].bitcast(I32), in_=g_words[g].rearrange("p n t -> p (n t)").bitcast(I32)[:, lo:hi])
+
+        def K():
+            nc.vector.tensor_copy(out=small_f[:], in_=small[:])
+            b, t = take()
+            nc.tensor.transpose(t[:, 0:P], small_f[:], ident[:])
+            nc.vector.tensor_copy(out=cols[:], in_=t[:, 0:20])
+            free.append(b)
+
+        def KB(h):
+            b, t = take()
+            for j in range(4):
+                nc.tensor.transpose(
+                    t[:, P * j : P * j + P], cols[:, 12 + 4 * h + j : 13 + 4 * h + j].to_broadcast([P, P]), ident[:]
+                )
+            nc.scalar.copy(out=theta_b[:, NT * h : NT * h + NT], in_=t[:])
+            free.append(b)
+
+        s_codes = {}
+        w_codes = {}
+        w_grp = {}
+        s_grp = {}
+        s_ord = {}
+        bank = {}
+
+        def R(j, g, eng="v"):
+            e = nc.vector.tensor_copy if eng == "v" else nc.scalar.copy
+            t = stage.tile([P, 4, P], F32, name="sord", tag="sord", bufs=SORD, align_bytes=64)
+            words = s_raw[j][:].rearrange("p a k -> p (a k)").bitcast(F32).rearrange("p (a g m u) -> p g a u m", a=2, g=3, u=2)
+            e(out=t[:].rearrange("p (a u) m -> p a u m", u=2), in_=words[:, g])
+            s_ord[j, g] = t
+
+        def T(j, g):
+            words = s_raw[j][:].rearrange("p a k -> p (a k)").bitcast(F32).rearrange("p (a k) -> p a k", a=2)
+            b, t = take()
+            for a in range(2):
+                for u in range(2):
+                    if (j, g) in s_ord:
+                        src = s_ord[j, g][:, 2 * a + u, :]
+                    else:
+                        src = words[:, a, 256 * g + u : 256 * (g + 1) : 2]
+                    c0 = P * (2 * a + u)
+                    nc.tensor.transpose(t[:, c0 : c0 + P], src, ident[:])
+            bank[j, g] = (b, t)
+
+        def C(j, g, eng="s"):
+            b, t = bank[j, g]
+            grp = stage.tile([P, 256, 4], BF16, name="sgrp", tag="sgrp", bufs=6, align_bytes=64)
+            e = nc.vector.tensor_copy if eng == "v" else nc.scalar.copy
+            e(
+                out=grp[:].rearrange("p n k -> p (n k)").bitcast(F32).rearrange("p (a r u) -> p a r u", a=2, u=2),
+                in_=t[:].rearrange("p (a u r) -> p a r u", a=2, u=2),
+            )
+            s_grp[j, g] = grp
+            free.append(b)
+
+        def Q(j, g):
+            codes = keep.tile([P, 256], U32, name="scode%d_%d" % (j, g), align_bytes=64)
+            plane = keep.tile([P, 256], U8, name="splane%d_%d" % (j, g), align_bytes=64)
+            nc.vector.quantize_mx(
+                out=codes[:].bitcast(E4M3), scales=plane[:], in_=s_grp[j, g][:].rearrange("p n k -> p (n k)")
+            )
+            s_codes[j, g] = (codes, plane)
+
+        def I(c, h, sc=S_COLS):
+            grp = stage.tile([P, NT, 4], BF16, name="wgrp", tag="wgrp", bufs=4, align_bytes=64)
+            raw = w_raw[c, h]
+            for eng, lo, hi in ((nc.scalar.copy, 0, sc), (nc.vector.tensor_copy, sc, NT)):
+                if hi > lo:
+                    eng(
+                        out=grp[:, lo:hi, :].rearrange("p (c i) t -> p c t i", i=4),
+                        in_=raw[:, :, lo:hi].rearrange("p t (c i) -> p c t i", i=4),
+                    )
+            w_grp[c, h] = grp
+
+        def W(c, h):
+            codes = keep.tile([P, NT], U32, name="wcode%d_%d" % (c, h), align_bytes=64)
+            plane = keep.tile([P, NT], U8, name="wplane%d_%d" % (c, h), align_bytes=64)
+            nc.vector.quantize_mx(
+                out=codes[:].bitcast(E4M3), scales=plane[:], in_=w_grp[c, h][:].rearrange("p w t -> p (w t)")
+            )
+            w_codes[c, h] = (codes, plane)
+
+        acc = {}
+
+        def M(n, c, h):
+            if c == 0:
+                acc[n, h] = take()
+            t = acc[n, h][1]
+            if c < 2:
+                cols_n = slice(P * n, P * n + P)
+                lhsT, lsc = g_codes[:, c, cols_n].bitcast(E5M2), g_plane[:, c, cols_n]
+            else:
+                codes, plane = s_codes[n // 2, c - 2]
+                cols_n = slice(P * (n % 2), P * (n % 2) + P)
+                lhsT, lsc = codes[:, cols_n].bitcast(E4M3), plane[:, cols_n]
+            wc, wp = w_codes[c, h]
+            nc.tensor.matmul_mx(
+                out=t[:], lhsT=lhsT, lhsT_scale=lsc, rhs=wc[:].bitcast(E4M3), rhs_scale=wp[:], start=(c == 0), stop=(c == 4)
+            )
+
+        def E(n, h):
+            b, t = acc[n, h]
+            o = stage.tile([P, NT], F32, name="o", tag="o", bufs=OUT_BUFS)
+            nc.vector.scalar_tensor_tensor(
+                out=o[:], in0=t[:], scalar=cols[:, n : n + 1], in1=theta_b[:, NT * h : NT * h + NT], op0=MULT, op1=ADD
+            )
+            free.append(b)
+            nc.sync.dma_start(out=out[P * n : P * n + P, NT * h : NT * h + NT], in_=o[:])
+
+        L_w(0, 0, 0, 256)
+        L_w(0, 0, 256, 512)
+        L_g(0, 0, 512)
+        load_planes()
+        L_s(0)
+        L_w(1, 0)
+        L_g(1, 0, 512)
+        L_w(2, 0)
+        L_s(1)
+        L_w(3, 0)
+        L_w(4, 0)
+        L_s(2)
+        L_g(0, 512, 1536)
+        L_g(1, 512, 1536)
+        L_s(3)
+        L_w(0, 1)
+        L_s(4)
+        L_w(1, 1)
+        L_w(2, 1)
+        L_s(5)
+        L_w(3, 1)
+        L_w(4, 1)
+        I(0, 0)
+        W(0, 0)
+        for n in range(4):
+            M(n, 0, 0)
+        I(1, 0, 192)
+        W(1, 0)
+        for g in range(3):
+            T(0, g)
+            C(0, g)
+        for g in range(3):
+            Q(0, g)
+        for n in range(4):
+            M(n, 1, 0)
+        I(2, 0, 192)
+        W(2, 0)
+        for n in range(2):
+            M(n, 2, 0)
+        K()
+        for g in range(3):
+            T(1, g)
+            C(1, g)
+        I(3, 0, 192)
+        W(3, 0)
+        for n in range(2):
+            M(n, 3, 0)
+        Q(1, 0)
+        Q(1, 1)
+        I(4, 0, 192)
+        W(4, 0)
+        Q(1, 2)
+        for c in (2, 3):
+            for n in (2, 3):
+                M(n, c, 0)
+        KB(0)
+        for g in range(3):
+            T(2, g)
+            C(2, g)
+        for g in range(3):
+            Q(2, g)
+        for n in range(4):
+            M(n, 4, 0)
+            E(n, 0)
+        KB(1)
+        for g in range(3):
+            T(3, g)
+            C(3, g)
+        for g in range(3):
+            Q(3, g)
+        for n in (4, 5):
+            for c in range(5):
+                M(n, c, 0)
+            E(n, 0)
+        for g in range(3):
+            T(4, g)
+            C(4, g)
+        for g in range(3):
+            Q(4, g)
+        I(0, 1, 320)
+        W(0, 1)
+        I(1, 1, 320)
+        W(1, 1)
+        for n in (6, 7):
+            for c in range(5):
+                M(n, c, 0)
+            E(n, 0)
+        for g in range(3):
+            T(5, g)
+            C(5, g)
+        for g in range(3):
+            Q(5, g)
+        I(2, 1, 320)
+        W(2, 1)
+        I(3, 1, 320)
+        W(3, 1)
+        I(4, 1, 320)
+        W(4, 1)
+        for n in (8, 9):
+            for c in range(5):
+                M(n, c, 0)
+            E(n, 0)
+        for n in (10, 11):
+            for c in range(5):
+                M(n, c, 0)
+            E(n, 0)
+        for n in range(12):
+            for c in range(5):
+                M(n, c, 1)
+            E(n, 1)
+
+
+OUT_BUFS = 12

@@ -20,7 +20,7 @@ N = 1536
 PAR = 1024
 NT = 512
 S_COLS = 256
-VPATH = []
+VPATH = [4,5]
 SORD = 6
 
 
@@ -32,7 +32,7 @@ def tile_score_influence_pseudovalues_e4_kernel(
         keep = ctx.enter_context(tc.tile_pool(name="keep", bufs=1))
         stage = ctx.enter_context(tc.tile_pool(name="stage", bufs=1))
         psum = ctx.enter_context(tc.psum_pool(name="psum", bufs=1))
-        ctx.enter_context(tc.manual_schedule(engines={mybir.EngineType.PE, mybir.EngineType.SP}))
+        ctx.enter_context(tc.manual_schedule())
 
         free = list(range(8))
 
@@ -53,10 +53,12 @@ def tile_score_influence_pseudovalues_e4_kernel(
         nc.vector.memset(small[:], 0.0)
         nc.vector.memset(g_plane[:].rearrange("p g n -> p (g n)").bitcast(I32), 0)
         w_rows = obs_weight.rearrange("(j p) -> j p", p=P)
-        def load_planes():
+        def load_small():
             nc.sync.dma_start(out=small[0:8, :], in_=w_rows[0:8, :])
             nc.sync.dma_start(out=small[8:12, :], in_=w_rows[8:12, :])
             nc.sync.dma_start(out=small[12:20, :], in_=theta.rearrange("(j p) -> j p", p=P))
+
+        def load_planes():
             for q in range(4):
                 nc.sync.dma_start(
                 out=g_plane[32 * q : 32 * q + 4, :, :].rearrange("p g n -> p (g n)").bitcast(I32).rearrange("p (g n) -> p g n", g=2),
@@ -74,8 +76,12 @@ def tile_score_influence_pseudovalues_e4_kernel(
             if j in VPATH:
                 x = t[:].rearrange("p a k -> p (a k)").rearrange("p (b k) -> p b k", b=8)
                 rows = score_eta[256 * j : 256 * j + 256, :].rearrange("(b r) k -> r b k", r=32)
-                for q in range(4):
-                    nc.sync.dma_start(out=x[32 * q : 32 * q + 32, :, :], in_=rows[:, :, 384 * q : 384 * q + 384])
+                for g in range(3):
+                    for q in range(4):
+                        k0 = 512 * g + 128 * q
+                        nc.sync.dma_start(
+                            out=x[32 * q : 32 * q + 32, :, 128 * g : 128 * g + 128], in_=rows[:, :, k0 : k0 + 128]
+                        )
             elif a is None:
                 nc.sync.dma_start(out=t[:], in_=rows)
             else:
@@ -120,8 +126,17 @@ def tile_score_influence_pseudovalues_e4_kernel(
         def R(j, g, eng="v"):
             e = nc.vector.tensor_copy if eng == "v" else nc.scalar.copy
             t = stage.tile([P, 4, P], F32, name="sord", tag="sord", bufs=SORD, align_bytes=64)
-            words = s_raw[j][:].rearrange("p a k -> p (a k)").bitcast(F32).rearrange("p (a g m u) -> p g a u m", a=2, g=3, u=2)
-            e(out=t[:].rearrange("p (a u) m -> p a u m", u=2), in_=words[:, g])
+            flat = s_raw[j][:].rearrange("p a k -> p (a k)").bitcast(F32)
+            if j in VPATH:
+                e(
+                    out=t[:].rearrange("p x m -> p (x m)").rearrange("p (b u c) -> p b u c", b=8, u=2),
+                    in_=flat.rearrange("p (b g c u) -> p g b u c", b=8, g=3, u=2)[:, g],
+                )
+            else:
+                e(
+                    out=t[:].rearrange("p (a u) m -> p a u m", u=2),
+                    in_=flat.rearrange("p (a g m u) -> p g a u m", a=2, g=3, u=2)[:, g],
+                )
             s_ord[j, g] = t
 
         def T(j, g):
@@ -136,6 +151,20 @@ def tile_score_influence_pseudovalues_e4_kernel(
                     c0 = P * (2 * a + u)
                     nc.tensor.transpose(t[:, c0 : c0 + P], src, ident[:])
             bank[j, g] = (b, t)
+
+        def V(j, g):
+            t = stage.tile([P, 512], F32, name="sturn", tag="sturn", bufs=3, align_bytes=64)
+            nc.vector.transpose(out=t[:], in_=s_ord[j, g][:].rearrange("p x c -> p (x c)"))
+            grp = stage.tile([P, 256, 4], BF16, name="sgrp", tag="sgrp", bufs=6, align_bytes=64)
+            s_grp[j, g] = grp
+            bank[j, g] = t
+
+        def Y(j, g, eng="s"):
+            e = nc.vector.tensor_copy if eng == "v" else nc.scalar.copy
+            e(
+                out=s_grp[j, g][:].rearrange("p n k -> p (n k)").bitcast(F32).rearrange("p (b r u) -> p b r u", b=8, u=2),
+                in_=bank[j, g][:].rearrange("p (b u r) -> p b r u", b=8, u=2),
+            )
 
         def C(j, g, eng="s"):
             b, t = bank[j, g]
@@ -167,6 +196,25 @@ def tile_score_influence_pseudovalues_e4_kernel(
                     )
             w_grp[c, h] = grp
 
+        def IG(c, h):
+            w_grp[c, h] = stage.tile([P, NT, 4], BF16, name="wgrp", tag="wgrp", bufs=4, align_bytes=64)
+
+        def IX(c, h, e, lo, hi):
+            e(
+                out=w_grp[c, h][:, lo:hi, :].rearrange("p (c i) t -> p c t i", i=4),
+                in_=w_raw[c, h][:, :, lo:hi].rearrange("p t (c i) -> p c t i", i=4),
+            )
+
+        def IS(c, h, sc=S_COLS):
+            if (c, h) not in w_grp:
+                IG(c, h)
+            IX(c, h, nc.scalar.copy, 0, sc)
+
+        def IV(c, h, sc=S_COLS):
+            if (c, h) not in w_grp:
+                IG(c, h)
+            IX(c, h, nc.vector.tensor_copy, sc, NT)
+
         def W(c, h):
             codes = keep.tile([P, NT], U32, name="wcode%d_%d" % (c, h), align_bytes=64)
             plane = keep.tile([P, NT], U8, name="wplane%d_%d" % (c, h), align_bytes=64)
@@ -176,6 +224,7 @@ def tile_score_influence_pseudovalues_e4_kernel(
             w_codes[c, h] = (codes, plane)
 
         acc = {}
+        outs = {}
 
         def M(n, c, h):
             if c == 0:
@@ -200,7 +249,10 @@ def tile_score_influence_pseudovalues_e4_kernel(
                 out=o[:], in0=t[:], scalar=cols[:, n : n + 1], in1=theta_b[:, NT * h : NT * h + NT], op0=MULT, op1=ADD
             )
             free.append(b)
-            nc.sync.dma_start(out=out[P * n : P * n + P, NT * h : NT * h + NT], in_=o[:])
+            outs[n, h] = o
+
+        def ST(n, h):
+            nc.sync.dma_start(out=out[P * n : P * n + P, NT * h : NT * h + NT], in_=outs[n, h][:])
 
         L_w(0, 0, 0, 256)
         L_w(0, 0, 256, 512)
@@ -208,110 +260,284 @@ def tile_score_influence_pseudovalues_e4_kernel(
         load_planes()
         L_s(0)
         L_w(1, 0)
+        IS(0, 0, 256)
         L_g(1, 0, 512)
+        IV(0, 0, 256)
         L_w(2, 0)
         L_s(1)
+        load_small()
+        W(0, 0)
         L_w(3, 0)
+        M(0, 0, 0)
+        M(1, 0, 0)
         L_w(4, 0)
+        M(2, 0, 0)
+        M(3, 0, 0)
+        T(0, 0)
+        IS(1, 0, 192)
+        IV(1, 0, 192)
         L_s(2)
+        T(0, 1)
         L_g(0, 512, 1536)
+        T(0, 2)
+        K()
+        C(0, 0)
+        W(1, 0)
+        C(0, 1)
+        Q(0, 0)
+        M(0, 1, 0)
         L_g(1, 512, 1536)
+        IV(2, 0, 192)
+        C(0, 2)
+        M(1, 1, 0)
+        IS(2, 0, 192)
+        Q(0, 1)
+        M(2, 1, 0)
+        Q(0, 2)
+        M(3, 1, 0)
         L_s(3)
         L_w(0, 1)
-        L_s(4)
+        W(2, 0)
         L_w(1, 1)
         L_w(2, 1)
-        L_s(5)
+        M(0, 2, 0)
+        M(1, 2, 0)
+        IS(3, 0, 192)
+        IV(3, 0, 192)
         L_w(3, 1)
-        L_w(4, 1)
-        I(0, 0)
-        W(0, 0)
-        for n in range(4):
-            M(n, 0, 0)
-        I(1, 0, 192)
-        W(1, 0)
-        for g in range(3):
-            T(0, g)
-            C(0, g)
-        for g in range(3):
-            Q(0, g)
-        for n in range(4):
-            M(n, 1, 0)
-        I(2, 0, 192)
-        W(2, 0)
-        for n in range(2):
-            M(n, 2, 0)
-        K()
-        for g in range(3):
-            T(1, g)
-            C(1, g)
-        I(3, 0, 192)
+        T(1, 0)
+        T(1, 1)
+        C(1, 0)
         W(3, 0)
-        for n in range(2):
-            M(n, 3, 0)
+        L_w(4, 1)
+        T(1, 2)
+        C(1, 1)
         Q(1, 0)
+        M(0, 3, 0)
+        IV(4, 0, 192)
+        C(1, 2)
+        M(1, 3, 0)
+        IS(4, 0, 192)
         Q(1, 1)
-        I(4, 0, 192)
-        W(4, 0)
         Q(1, 2)
-        for c in (2, 3):
-            for n in (2, 3):
-                M(n, c, 0)
         KB(0)
-        for g in range(3):
-            T(2, g)
-            C(2, g)
-        for g in range(3):
-            Q(2, g)
-        for n in range(4):
-            M(n, 4, 0)
-            E(n, 0)
         KB(1)
-        for g in range(3):
-            T(3, g)
-            C(3, g)
-        for g in range(3):
-            Q(3, g)
-        for n in (4, 5):
-            for c in range(5):
-                M(n, c, 0)
-            E(n, 0)
-        for g in range(3):
-            T(4, g)
-            C(4, g)
-        for g in range(3):
-            Q(4, g)
-        I(0, 1, 320)
+        W(4, 0)
+        M(2, 2, 0)
+        M(3, 2, 0)
+        M(2, 3, 0)
+        M(3, 3, 0)
+        T(2, 0)
+        T(2, 1)
+        C(2, 0)
+        T(2, 2)
+        C(2, 1)
+        Q(2, 0)
+        M(0, 4, 0)
+        C(2, 2)
+        Q(2, 1)
+        M(1, 4, 0)
+        M(2, 4, 0)
+        E(0, 0)
+        M(3, 4, 0)
+        T(3, 0)
+        Q(2, 2)
+        IS(0, 1, 384)
+        ST(0, 0)
+        E(1, 0)
+        T(3, 1)
+        E(2, 0)
+        ST(1, 0)
+        T(3, 2)
+        E(3, 0)
+        M(4, 0, 0)
+        ST(2, 0)
+        C(3, 0)
+        M(4, 1, 0)
+        IV(0, 1, 384)
+        ST(3, 0)
+        M(4, 2, 0)
+        IV(1, 1, 384)
+        C(3, 1)
+        M(4, 3, 0)
+        Q(3, 0)
+        M(4, 4, 0)
+        C(3, 2)
+        M(5, 0, 0)
         W(0, 1)
-        I(1, 1, 320)
+        M(5, 1, 0)
+        IS(1, 1, 384)
+        M(5, 2, 0)
+        Q(3, 1)
+        M(5, 3, 0)
+        Q(3, 2)
+        M(5, 4, 0)
+        E(4, 0)
+        M(6, 0, 0)
+        M(6, 1, 0)
+        E(5, 0)
+        M(6, 2, 0)
+        ST(4, 0)
+        L_s(4)
+        M(6, 3, 0)
+        IS(2, 1, 384)
+        IV(2, 1, 384)
+        M(6, 4, 0)
+        M(7, 0, 0)
         W(1, 1)
-        for n in (6, 7):
-            for c in range(5):
-                M(n, c, 0)
-            E(n, 0)
-        for g in range(3):
-            T(5, g)
-            C(5, g)
-        for g in range(3):
-            Q(5, g)
-        I(2, 1, 320)
+        M(7, 1, 0)
+        M(7, 2, 0)
+        E(6, 0)
+        M(7, 3, 0)
+        M(7, 4, 0)
+        IV(3, 1, 384)
+        M(0, 0, 1)
+        IS(3, 1, 384)
+        M(1, 0, 1)
+        E(7, 0)
+        M(2, 0, 1)
+        M(3, 0, 1)
         W(2, 1)
-        I(3, 1, 320)
+        M(4, 0, 1)
+        M(5, 0, 1)
+        IV(4, 1, 384)
+        M(6, 0, 1)
+        ST(5, 0)
+        ST(6, 0)
+        M(7, 0, 1)
+        IS(4, 1, 384)
+        M(0, 1, 1)
         W(3, 1)
-        I(4, 1, 320)
+        M(1, 1, 1)
+        L_s(5)
+        M(2, 1, 1)
+        M(3, 1, 1)
+        M(4, 1, 1)
+        M(5, 1, 1)
+        M(6, 1, 1)
+        R(4, 0, "s")
+        M(7, 1, 1)
         W(4, 1)
-        for n in (8, 9):
-            for c in range(5):
-                M(n, c, 0)
-            E(n, 0)
-        for n in (10, 11):
-            for c in range(5):
-                M(n, c, 0)
-            E(n, 0)
-        for n in range(12):
-            for c in range(5):
-                M(n, c, 1)
-            E(n, 1)
+        M(0, 2, 1)
+        M(1, 2, 1)
+        R(4, 1, "s")
+        V(4, 0)
+        M(2, 2, 1)
+        M(3, 2, 1)
+        R(4, 2, "s")
+        M(4, 2, 1)
+        V(4, 1)
+        M(5, 2, 1)
+        M(6, 2, 1)
+        Y(4, 0, "s")
+        V(4, 2)
+        M(7, 2, 1)
+        M(0, 3, 1)
+        ST(7, 0)
+        Y(4, 1, "s")
+        M(1, 3, 1)
+        Q(4, 0)
+        M(2, 3, 1)
+        M(3, 3, 1)
+        Y(4, 2, "s")
+        Q(4, 1)
+        M(4, 3, 1)
+        M(5, 3, 1)
+        R(5, 0, "s")
+        M(6, 3, 1)
+        Q(4, 2)
+        M(7, 3, 1)
+        M(0, 4, 1)
+        R(5, 1, "s")
+        V(5, 0)
+        M(1, 4, 1)
+        M(2, 4, 1)
+        R(5, 2, "s")
+        E(0, 1)
+        M(3, 4, 1)
+        M(4, 4, 1)
+        E(1, 1)
+        Y(5, 0, "s")
+        M(5, 4, 1)
+        ST(0, 1)
+        M(6, 4, 1)
+        E(2, 1)
+        M(7, 4, 1)
+        ST(1, 1)
+        M(8, 0, 0)
+        M(8, 1, 0)
+        E(3, 1)
+        ST(2, 1)
+        M(8, 2, 0)
+        M(8, 3, 0)
+        V(5, 1)
+        ST(3, 1)
+        M(8, 4, 0)
+        M(8, 0, 1)
+        V(5, 2)
+        Y(5, 1, "s")
+        M(8, 1, 1)
+        M(8, 2, 1)
+        Q(5, 0)
+        M(8, 3, 1)
+        Y(5, 2, "s")
+        E(4, 1)
+        M(8, 4, 1)
+        M(9, 0, 0)
+        Q(5, 1)
+        M(9, 1, 0)
+        ST(4, 1)
+        Q(5, 2)
+        M(9, 2, 0)
+        M(9, 3, 0)
+        E(5, 1)
+        M(9, 4, 0)
+        M(9, 0, 1)
+        E(6, 1)
+        ST(5, 1)
+        M(9, 1, 1)
+        M(9, 2, 1)
+        E(7, 1)
+        ST(6, 1)
+        M(9, 3, 1)
+        M(9, 4, 1)
+        E(8, 0)
+        ST(7, 1)
+        M(10, 0, 0)
+        M(10, 1, 0)
+        E(8, 1)
+        ST(8, 0)
+        M(10, 2, 0)
+        M(10, 3, 0)
+        E(9, 0)
+        M(10, 4, 0)
+        ST(8, 1)
+        M(10, 0, 1)
+        E(9, 1)
+        M(10, 1, 1)
+        ST(9, 0)
+        M(10, 2, 1)
+        E(10, 0)
+        M(10, 3, 1)
+        ST(9, 1)
+        M(10, 4, 1)
+        M(11, 0, 0)
+        ST(10, 0)
+        E(10, 1)
+        M(11, 1, 0)
+        M(11, 2, 0)
+        M(11, 3, 0)
+        ST(10, 1)
+        M(11, 4, 0)
+        M(11, 0, 1)
+        E(11, 0)
+        M(11, 1, 1)
+        M(11, 2, 1)
+        M(11, 3, 1)
+        ST(11, 0)
+        M(11, 4, 1)
+        E(11, 1)
+        ST(11, 1)
 
 
 OUT_BUFS = 12

@@ -97,15 +97,44 @@ def tile_score_influence_pseudovalues_e4_kernel(
             else:
                 nc.sync.dma_start(out=t[:, :, lo:hi], in_=v_et[512 * (c - 2) : 512 * (c - 1), wc].rearrange("(p j) w -> p j w", j=4))
 
+        def L_v():
+            t = keep.tile([P, 2, 8, 384], BF16, name="sraw45", align_bytes=64)
+            rows = score_eta[1024:1536, :].rearrange("(b r) k -> r b k", r=32)
+            x = t[:].rearrange("p j b k -> p (j b) k")
+            for g in range(3):
+                for q in range(4):
+                    k0 = 512 * g + 128 * q
+                    nc.sync.dma_start(out=x[32 * q : 32 * q + 32, :, 128 * g : 128 * g + 128], in_=rows[:, :, k0 : k0 + 128])
+            for j in range(2):
+                s_raw[4 + j] = t[:, j, :, :]
+
+        def L_f(c, part=None):
+            t = keep.tile([P, 4, PAR], BF16, name="wfull%d" % c, align_bytes=64)
+            src = v_tt[512 * c : 512 * c + 512] if c < 2 else v_et[512 * (c - 2) : 512 * (c - 1)]
+            src = src.rearrange("(p j) w -> p j w", j=4)
+            if part is None:
+                nc.sync.dma_start(out=t[:], in_=src)
+            else:
+                nc.sync.dma_start(out=t[:, :, 0:part], in_=src[:, :, 0:part])
+                nc.sync.dma_start(out=t[:, :, part:PAR], in_=src[:, :, part:PAR])
+            for h in range(2):
+                w_raw[c, h] = t[:, :, NT * h : NT * h + NT]
+
         def L_g(g, lo, hi):
             nc.sync.dma_start(out=g_codes[:, g, lo:hi].bitcast(I32), in_=g_words[g].rearrange("p n t -> p (n t)").bitcast(I32)[:, lo:hi])
 
-        def K():
+        kb = {}
+
+        def KA():
             nc.vector.tensor_copy(out=small_f[:], in_=small[:])
-            b, t = take()
-            nc.tensor.transpose(t[:, 0:P], small_f[:], ident[:])
-            nc.vector.tensor_copy(out=cols[:], in_=t[:, 0:20])
-            free.append(b)
+
+        def KT():
+            kb[0] = take()
+            nc.tensor.transpose(kb[0][1][:, 0:P], small_f[:], ident[:])
+
+        def KC():
+            nc.vector.tensor_copy(out=cols[:], in_=kb[0][1][:, 0:20])
+            free.append(kb[0][0])
 
         def KB(h):
             b, t = take()
@@ -113,6 +142,10 @@ def tile_score_influence_pseudovalues_e4_kernel(
                 nc.tensor.transpose(
                     t[:, P * j : P * j + P], cols[:, 12 + 4 * h + j : 13 + 4 * h + j].to_broadcast([P, P]), ident[:]
                 )
+            kb[1 + h] = (b, t)
+
+        def KD(h):
+            b, t = kb[1 + h]
             nc.scalar.copy(out=theta_b[:, NT * h : NT * h + NT], in_=t[:])
             free.append(b)
 
@@ -126,16 +159,15 @@ def tile_score_influence_pseudovalues_e4_kernel(
         def R(j, g, eng="v"):
             e = nc.vector.tensor_copy if eng == "v" else nc.scalar.copy
             t = stage.tile([P, 4, P], F32, name="sord", tag="sord", bufs=SORD, align_bytes=64)
-            flat = s_raw[j][:].rearrange("p a k -> p (a k)").bitcast(F32)
             if j in VPATH:
                 e(
                     out=t[:].rearrange("p x m -> p (x m)").rearrange("p (b u c) -> p b u c", b=8, u=2),
-                    in_=flat.rearrange("p (b g c u) -> p g b u c", b=8, g=3, u=2)[:, g],
+                    in_=s_raw[j].rearrange("p b k -> p (b k)").bitcast(F32).rearrange("p (b g c u) -> p g b u c", b=8, g=3, u=2)[:, g],
                 )
             else:
                 e(
                     out=t[:].rearrange("p (a u) m -> p a u m", u=2),
-                    in_=flat.rearrange("p (a g m u) -> p g a u m", a=2, g=3, u=2)[:, g],
+                    in_=s_raw[j][:].rearrange("p a k -> p (a k)").bitcast(F32).rearrange("p (a g m u) -> p g a u m", a=2, g=3, u=2)[:, g],
                 )
             s_ord[j, g] = t
 
@@ -205,6 +237,28 @@ def tile_score_influence_pseudovalues_e4_kernel(
                 in_=w_raw[c, h][:, :, lo:hi].rearrange("p t (c i) -> p c t i", i=4),
             )
 
+        def HS(c, h, q, n):
+            if (c, h) not in w_grp:
+                IG(c, h)
+            IX(c, h, nc.scalar.copy, 256 * q, 256 * q + n)
+
+        def HV(c, h, q, n):
+            if (c, h) not in w_grp:
+                IG(c, h)
+            IX(c, h, nc.vector.tensor_copy, 256 * q + n, 256 * q + 256)
+
+        def HW(c, h, q):
+            if (c, h) not in w_codes:
+                w_codes[c, h] = (
+                    keep.tile([P, NT], U32, name="wcode%d_%d" % (c, h), align_bytes=64),
+                    keep.tile([P, NT], U8, name="wplane%d_%d" % (c, h), align_bytes=64),
+                )
+            codes, plane = w_codes[c, h]
+            s = slice(256 * q, 256 * q + 256)
+            nc.vector.quantize_mx(
+                out=codes[:, s].bitcast(E4M3), scales=plane[:, s], in_=w_grp[c, h][:, s, :].rearrange("p w t -> p (w t)")
+            )
+
         def IS(c, h, sc=S_COLS):
             if (c, h) not in w_grp:
                 IG(c, h)
@@ -224,11 +278,14 @@ def tile_score_influence_pseudovalues_e4_kernel(
             w_codes[c, h] = (codes, plane)
 
         acc = {}
+        cnt = {}
         outs = {}
 
         def M(n, c, h):
-            if c == 0:
+            if (n, h) not in acc:
                 acc[n, h] = take()
+                cnt[n, h] = 0
+            cnt[n, h] += 1
             t = acc[n, h][1]
             if c < 2:
                 cols_n = slice(P * n, P * n + P)
@@ -239,7 +296,7 @@ def tile_score_influence_pseudovalues_e4_kernel(
                 lhsT, lsc = codes[:, cols_n].bitcast(E4M3), plane[:, cols_n]
             wc, wp = w_codes[c, h]
             nc.tensor.matmul_mx(
-                out=t[:], lhsT=lhsT, lhsT_scale=lsc, rhs=wc[:].bitcast(E4M3), rhs_scale=wp[:], start=(c == 0), stop=(c == 4)
+                out=t[:], lhsT=lhsT, lhsT_scale=lsc, rhs=wc[:].bitcast(E4M3), rhs_scale=wp[:], start=(cnt[n, h] == 1), stop=(cnt[n, h] == 5)
             )
 
         def E(n, h):
@@ -251,6 +308,17 @@ def tile_score_influence_pseudovalues_e4_kernel(
             free.append(b)
             outs[n, h] = o
 
+        def EH(n, h):
+            b, t = acc[n, h]
+            for q in range(2):
+                lo = 256 * q
+                o = stage.tile([P, 256], F32, name="oh", tag="oh", bufs=2)
+                nc.vector.scalar_tensor_tensor(
+                    out=o[:], in0=t[:, lo : lo + 256], scalar=cols[:, n : n + 1],
+                    in1=theta_b[:, NT * h + lo : NT * h + lo + 256], op0=MULT, op1=ADD,
+                )
+                nc.sync.dma_start(out=out[P * n : P * n + P, NT * h + lo : NT * h + lo + 256], in_=o[:])
+
         def ST(n, h):
             nc.sync.dma_start(out=out[P * n : P * n + P, NT * h : NT * h + NT], in_=outs[n, h][:])
 
@@ -260,284 +328,292 @@ def tile_score_influence_pseudovalues_e4_kernel(
         load_planes()
         L_s(0)
         L_w(1, 0)
-        IS(0, 0, 256)
         L_g(1, 0, 512)
-        IV(0, 0, 256)
         L_w(2, 0)
         L_s(1)
         load_small()
-        W(0, 0)
         L_w(3, 0)
+        L_w(4, 0)
+        L_s(2)
+        L_g(0, 512, 1536)
+        L_g(1, 512, 1536)
+        L_s(3)
+        L_w(0, 1)
+        L_w(1, 1)
+        L_w(2, 1)
+        L_w(3, 1)
+        L_w(4, 1)
+        L_v()
+        HS(0, 0, 0, 128)
+        HV(0, 0, 0, 128)
+        HW(0, 0, 0)
+        HS(0, 0, 1, 96)
+        HV(0, 0, 1, 96)
+        HW(0, 0, 1)
         M(0, 0, 0)
         M(1, 0, 0)
-        L_w(4, 0)
         M(2, 0, 0)
         M(3, 0, 0)
         T(0, 0)
-        IS(1, 0, 192)
-        IV(1, 0, 192)
-        L_s(2)
         T(0, 1)
-        L_g(0, 512, 1536)
         T(0, 2)
-        K()
+        IS(1, 0, 128)
+        IV(1, 0, 128)
         C(0, 0)
-        W(1, 0)
         C(0, 1)
-        Q(0, 0)
-        M(0, 1, 0)
-        L_g(1, 512, 1536)
-        IV(2, 0, 192)
         C(0, 2)
+        W(1, 0)
+        M(0, 1, 0)
         M(1, 1, 0)
-        IS(2, 0, 192)
-        Q(0, 1)
         M(2, 1, 0)
-        Q(0, 2)
         M(3, 1, 0)
-        L_s(3)
-        L_w(0, 1)
+        Q(0, 0)
+        Q(0, 1)
+        IS(2, 0, 128)
+        IV(2, 0, 128)
+        Q(0, 2)
         W(2, 0)
-        L_w(1, 1)
-        L_w(2, 1)
         M(0, 2, 0)
         M(1, 2, 0)
-        IS(3, 0, 192)
-        IV(3, 0, 192)
-        L_w(3, 1)
+        KA()
+        IS(3, 0, 128)
+        IV(3, 0, 128)
         T(1, 0)
         T(1, 1)
-        C(1, 0)
-        W(3, 0)
-        L_w(4, 1)
         T(1, 2)
+        KT()
+        W(3, 0)
+        C(1, 0)
         C(1, 1)
-        Q(1, 0)
-        M(0, 3, 0)
-        IV(4, 0, 192)
         C(1, 2)
+        Q(1, 0)
+        KC()
+        IS(4, 0, 128)
+        IV(4, 0, 128)
+        M(0, 3, 0)
         M(1, 3, 0)
-        IS(4, 0, 192)
         Q(1, 1)
-        Q(1, 2)
-        KB(0)
-        KB(1)
         W(4, 0)
+        Q(1, 2)
         M(2, 2, 0)
         M(3, 2, 0)
         M(2, 3, 0)
         M(3, 3, 0)
+        R(2, 0, "s")
+        R(2, 1, "s")
+        R(2, 2, "s")
+        KB(0)
+        KD(0)
+        KB(1)
+        KD(1)
         T(2, 0)
         T(2, 1)
-        C(2, 0)
         T(2, 2)
+        C(2, 0)
         C(2, 1)
-        Q(2, 0)
-        M(0, 4, 0)
         C(2, 2)
-        Q(2, 1)
+        M(0, 4, 0)
         M(1, 4, 0)
         M(2, 4, 0)
-        E(0, 0)
         M(3, 4, 0)
-        T(3, 0)
-        Q(2, 2)
-        IS(0, 1, 384)
+        E(0, 0)
         ST(0, 0)
-        E(1, 0)
+        Q(2, 0)
+        Q(2, 1)
+        T(3, 0)
         T(3, 1)
-        E(2, 0)
-        ST(1, 0)
         T(3, 2)
-        E(3, 0)
-        M(4, 0, 0)
+        E(1, 0)
+        ST(1, 0)
+        Q(2, 2)
+        E(2, 0)
         ST(2, 0)
-        C(3, 0)
-        M(4, 1, 0)
-        IV(0, 1, 384)
+        E(3, 0)
         ST(3, 0)
-        M(4, 2, 0)
-        IV(1, 1, 384)
+        C(3, 0)
+        IS(0, 1, 384)
+        IV(0, 1, 384)
         C(3, 1)
-        M(4, 3, 0)
-        Q(3, 0)
-        M(4, 4, 0)
         C(3, 2)
-        M(5, 0, 0)
-        W(0, 1)
-        M(5, 1, 0)
         IS(1, 1, 384)
+        IV(1, 1, 384)
+        Q(3, 0)
+        W(0, 1)
+        M(4, 0, 0)
+        M(4, 1, 0)
+        M(4, 2, 0)
+        M(4, 3, 0)
+        M(4, 4, 0)
+        M(5, 0, 0)
+        M(5, 1, 0)
         M(5, 2, 0)
-        Q(3, 1)
         M(5, 3, 0)
-        Q(3, 2)
         M(5, 4, 0)
+        Q(3, 1)
+        Q(3, 2)
         E(4, 0)
-        M(6, 0, 0)
-        M(6, 1, 0)
-        E(5, 0)
-        M(6, 2, 0)
         ST(4, 0)
-        L_s(4)
-        M(6, 3, 0)
+        E(5, 0)
+        ST(5, 0)
         IS(2, 1, 384)
         IV(2, 1, 384)
+        M(6, 0, 0)
+        M(6, 1, 0)
+        M(6, 2, 0)
+        M(6, 3, 0)
         M(6, 4, 0)
         M(7, 0, 0)
-        W(1, 1)
         M(7, 1, 0)
         M(7, 2, 0)
-        E(6, 0)
         M(7, 3, 0)
         M(7, 4, 0)
-        IV(3, 1, 384)
-        M(0, 0, 1)
+        W(1, 1)
+        E(6, 0)
+        ST(6, 0)
         IS(3, 1, 384)
-        M(1, 0, 1)
+        IV(3, 1, 384)
         E(7, 0)
+        ST(7, 0)
+        W(2, 1)
+        IS(4, 1, 384)
+        IV(4, 1, 384)
+        W(3, 1)
+        W(4, 1)
+        M(0, 0, 1)
+        M(1, 0, 1)
         M(2, 0, 1)
         M(3, 0, 1)
-        W(2, 1)
         M(4, 0, 1)
         M(5, 0, 1)
-        IV(4, 1, 384)
         M(6, 0, 1)
-        ST(5, 0)
-        ST(6, 0)
         M(7, 0, 1)
-        IS(4, 1, 384)
         M(0, 1, 1)
-        W(3, 1)
         M(1, 1, 1)
-        L_s(5)
         M(2, 1, 1)
         M(3, 1, 1)
         M(4, 1, 1)
         M(5, 1, 1)
         M(6, 1, 1)
-        R(4, 0, "s")
         M(7, 1, 1)
-        W(4, 1)
         M(0, 2, 1)
         M(1, 2, 1)
-        R(4, 1, "s")
-        V(4, 0)
         M(2, 2, 1)
         M(3, 2, 1)
-        R(4, 2, "s")
         M(4, 2, 1)
-        V(4, 1)
         M(5, 2, 1)
         M(6, 2, 1)
-        Y(4, 0, "s")
-        V(4, 2)
         M(7, 2, 1)
         M(0, 3, 1)
-        ST(7, 0)
-        Y(4, 1, "s")
         M(1, 3, 1)
-        Q(4, 0)
         M(2, 3, 1)
         M(3, 3, 1)
-        Y(4, 2, "s")
-        Q(4, 1)
         M(4, 3, 1)
         M(5, 3, 1)
-        R(5, 0, "s")
         M(6, 3, 1)
-        Q(4, 2)
         M(7, 3, 1)
-        M(0, 4, 1)
+        R(4, 0, "s")
+        R(4, 1, "s")
+        R(4, 2, "s")
+        V(4, 0)
+        V(4, 1)
+        V(4, 2)
+        Y(4, 0, "s")
+        Y(4, 1, "s")
+        Y(4, 2, "s")
+        R(5, 0, "s")
         R(5, 1, "s")
-        V(5, 0)
-        M(1, 4, 1)
-        M(2, 4, 1)
         R(5, 2, "s")
+        Q(4, 0)
+        Q(4, 1)
+        Q(4, 2)
+        M(0, 4, 1)
         E(0, 1)
-        M(3, 4, 1)
-        M(4, 4, 1)
-        E(1, 1)
-        Y(5, 0, "s")
-        M(5, 4, 1)
         ST(0, 1)
-        M(6, 4, 1)
-        E(2, 1)
-        M(7, 4, 1)
+        M(1, 4, 1)
+        E(1, 1)
         ST(1, 1)
+        M(2, 4, 1)
+        E(2, 1)
+        ST(2, 1)
+        M(3, 4, 1)
+        E(3, 1)
+        ST(3, 1)
+        V(5, 0)
+        Y(5, 0, "s")
+        M(4, 4, 1)
+        E(4, 1)
+        ST(4, 1)
+        V(5, 1)
+        Y(5, 1, "s")
+        M(5, 4, 1)
+        E(5, 1)
+        ST(5, 1)
+        V(5, 2)
+        Y(5, 2, "s")
+        Q(5, 0)
+        M(6, 4, 1)
+        E(6, 1)
+        ST(6, 1)
+        Q(5, 1)
+        M(7, 4, 1)
+        E(7, 1)
+        ST(7, 1)
+        Q(5, 2)
         M(8, 0, 0)
         M(8, 1, 0)
-        E(3, 1)
-        ST(2, 1)
         M(8, 2, 0)
         M(8, 3, 0)
-        V(5, 1)
-        ST(3, 1)
         M(8, 4, 0)
+        E(8, 0)
+        ST(8, 0)
         M(8, 0, 1)
-        V(5, 2)
-        Y(5, 1, "s")
         M(8, 1, 1)
         M(8, 2, 1)
-        Q(5, 0)
         M(8, 3, 1)
-        Y(5, 2, "s")
-        E(4, 1)
         M(8, 4, 1)
+        E(8, 1)
+        ST(8, 1)
         M(9, 0, 0)
-        Q(5, 1)
         M(9, 1, 0)
-        ST(4, 1)
-        Q(5, 2)
         M(9, 2, 0)
         M(9, 3, 0)
-        E(5, 1)
         M(9, 4, 0)
+        E(9, 0)
+        ST(9, 0)
         M(9, 0, 1)
-        E(6, 1)
-        ST(5, 1)
         M(9, 1, 1)
         M(9, 2, 1)
-        E(7, 1)
-        ST(6, 1)
         M(9, 3, 1)
         M(9, 4, 1)
-        E(8, 0)
-        ST(7, 1)
+        E(9, 1)
+        ST(9, 1)
         M(10, 0, 0)
         M(10, 1, 0)
-        E(8, 1)
-        ST(8, 0)
         M(10, 2, 0)
         M(10, 3, 0)
-        E(9, 0)
         M(10, 4, 0)
-        ST(8, 1)
-        M(10, 0, 1)
-        E(9, 1)
-        M(10, 1, 1)
-        ST(9, 0)
-        M(10, 2, 1)
         E(10, 0)
-        M(10, 3, 1)
-        ST(9, 1)
-        M(10, 4, 1)
-        M(11, 0, 0)
         ST(10, 0)
+        M(10, 0, 1)
+        M(10, 1, 1)
+        M(10, 2, 1)
+        M(10, 3, 1)
+        M(10, 4, 1)
         E(10, 1)
+        ST(10, 1)
+        M(11, 0, 0)
         M(11, 1, 0)
         M(11, 2, 0)
         M(11, 3, 0)
-        ST(10, 1)
         M(11, 4, 0)
-        M(11, 0, 1)
         E(11, 0)
+        ST(11, 0)
+        M(11, 0, 1)
         M(11, 1, 1)
         M(11, 2, 1)
         M(11, 3, 1)
-        ST(11, 0)
         M(11, 4, 1)
-        E(11, 1)
-        ST(11, 1)
+        EH(11, 1)
 
 
 OUT_BUFS = 12

from contextlib import ExitStack

import concourse.mybir as mybir
from concourse.masks import make_identity

FLOPS = 2 * 1536 * 1024 * (1024 + 1536)

F32 = mybir.dt.float32
BF16 = mybir.dt.bfloat16
I32 = mybir.dt.int32
U32 = mybir.dt.uint32
U8 = mybir.dt.uint8
E4M3 = mybir.dt.float8_e4m3fn_x4
E5M2 = mybir.dt.float8_e5m2_x4
MULT = mybir.AluOpType.mult
ADD = mybir.AluOpType.add

P = 128
N = 1536
PAR = 1024
NT = 512
S_COLS = 256
VPATH = [4,5]
SORD = 6


def tile_score_influence_pseudovalues_e4_kernel(
    tc, g_words, g_scales, v_tt, score_eta, v_et, obs_weight, theta, out
):
    nc = tc.nc
    with ExitStack() as ctx:
        keep = ctx.enter_context(tc.tile_pool(name="keep", bufs=1))
        stage = ctx.enter_context(tc.tile_pool(name="stage", bufs=1))
        psum = ctx.enter_context(tc.psum_pool(name="psum", bufs=1))
        ctx.enter_context(tc.manual_schedule())

        free = list(range(8))

        def take():
            b = free.pop(0)
            return b, psum.tile([P, NT], F32, name="bank%d" % b, tag="bank%d" % b, bufs=1)

        small = keep.tile([P, P], BF16, name="small")
        small_f = keep.tile([P, P], F32, name="small_f")
        cols = keep.tile([P, 20], F32, name="cols")
        theta_b = keep.tile([P, PAR], F32, name="theta_b")
        ident = keep.tile([P, P], F32, name="ident")
        g_codes = keep.tile([P, 2, N], U32, name="g_codes", align_bytes=64)
        g_plane = keep.tile([P, 2, N], U8, name="g_plane", align_bytes=64)


        make_identity(nc, ident[:])
        nc.vector.memset(small[:], 0.0)
        nc.vector.memset(g_plane[:].rearrange("p g n -> p (g n)").bitcast(I32), 0)
        w_rows = obs_weight.rearrange("(j p) -> j p", p=P)
        def load_small():
            nc.sync.dma_start(out=small[0:8, :], in_=w_rows[0:8, :])
            nc.sync.dma_start(out=small[8:12, :], in_=w_rows[8:12, :])
            nc.sync.dma_start(out=small[12:20, :], in_=theta.rearrange("(j p) -> j p", p=P))

        def load_planes():
            for q in range(4):
                nc.sync.dma_start(
                out=g_plane[32 * q : 32 * q + 4, :, :].rearrange("p g n -> p (g n)").bitcast(I32).rearrange("p (g n) -> p g n", g=2),
                in_=g_scales[:, 4 * q : 4 * q + 4, :].bitcast(I32).rearrange("g r n -> r g n"),
                )
        s_raw = {}
        w_raw = {}

        def L_s(j, a=None):
            if j not in s_raw:
                t = keep.tile([P, 2, N], BF16, name="sraw%d" % j, align_bytes=64)
                s_raw[j] = t
            t = s_raw[j]
            rows = score_eta[256 * j : 256 * j + 256, :].rearrange("(a p) k -> p a k", p=P)
            if j in VPATH:
                x = t[:].rearrange("p a k -> p (a k)").rearrange("p (b k) -> p b k", b=8)
                rows = score_eta[256 * j : 256 * j + 256, :].rearrange("(b r) k -> r b k", r=32)
                for g in range(3):
                    for q in range(4):
                        k0 = 512 * g + 128 * q
                        nc.sync.dma_start(
                            out=x[32 * q : 32 * q + 32, :, 128 * g : 128 * g + 128], in_=rows[:, :, k0 : k0 + 128]
                        )
            elif a is None:
                nc.sync.dma_start(out=t[:], in_=rows)
            else:
                nc.sync.dma_start(out=t[:, a, :], in_=rows[:, a, :])

        def L_w(c, h, lo=0, hi=NT):
            if (c, h) not in w_raw:
                w_raw[c, h] = keep.tile([P, 4, NT], BF16, name="wraw%d_%d" % (c, h), align_bytes=64)
            t = w_raw[c, h]
            wc = slice(NT * h + lo, NT * h + hi)
            if c < 2:
                nc.sync.dma_start(out=t[:, :, lo:hi], in_=v_tt[512 * c : 512 * c + 512, wc].rearrange("(p j) w -> p j w", j=4))
            else:
                nc.sync.dma_start(out=t[:, :, lo:hi], in_=v_et[512 * (c - 2) : 512 * (c - 1), wc].rearrange("(p j) w -> p j w", j=4))

        def L_v():
            t = keep.tile([P, 2, 8, 384], BF16, name="sraw45", align_bytes=64)
            rows = score_eta[1024:1536, :].rearrange("(b r) k -> r b k", r=32)
            x = t[:].rearrange("p j b k -> p (j b) k")
            for g in range(3):
                for q in range(4):
                    k0 = 512 * g + 128 * q
                    nc.sync.dma_start(out=x[32 * q : 32 * q + 32, :, 128 * g : 128 * g + 128], in_=rows[:, :, k0 : k0 + 128])
            for j in range(2):
                s_raw[4 + j] = t[:, j, :, :]

        def L_f(c, part=None):
            t = keep.tile([P, 4, PAR], BF16, name="wfull%d" % c, align_bytes=64)
            src = v_tt[512 * c : 512 * c + 512] if c < 2 else v_et[512 * (c - 2) : 512 * (c - 1)]
            src = src.rearrange("(p j) w -> p j w", j=4)
            if part is None:
                nc.sync.dma_start(out=t[:], in_=src)
            else:
                nc.sync.dma_start(out=t[:, :, 0:part], in_=src[:, :, 0:part])
                nc.sync.dma_start(out=t[:, :, part:PAR], in_=src[:, :, part:PAR])
            for h in range(2):
                w_raw[c, h] = t[:, :, NT * h : NT * h + NT]

        def L_g(g, lo, hi):
            nc.sync.dma_start(out=g_codes[:, g, lo:hi].bitcast(I32), in_=g_words[g].rearrange("p n t -> p (n t)").bitcast(I32)[:, lo:hi])

        kb = {}

        def KA():
            nc.vector.tensor_copy(out=small_f[:], in_=small[:])

        def KT():
            kb[0] = take()
            nc.tensor.transpose(kb[0][1][:, 0:P], small_f[:], ident[:])

        def KC():
            nc.vector.tensor_copy(out=cols[:], in_=kb[0][1][:, 0:20])
            free.append(kb[0][0])

        def KB(h):
            b, t = take()
            for j in range(4):
                nc.tensor.transpose(
                    t[:, P * j : P * j + P], cols[:, 12 + 4 * h + j : 13 + 4 * h + j].to_broadcast([P, P]), ident[:]
                )
            kb[1 + h] = (b, t)

        def KD(h):
            b, t = kb[1 + h]
            nc.scalar.copy(out=theta_b[:, NT * h : NT * h + NT], in_=t[:])
            free.append(b)

        s_codes = {}
        w_codes = {}
        w_grp = {}
        s_grp = {}
        s_ord = {}
        bank = {}

        def R(j, g, eng="v"):
            e = nc.vector.tensor_copy if eng == "v" else nc.scalar.copy
            t = stage.tile([P, 4, P], F32, name="sord", tag="sord", bufs=SORD, align_bytes=64)
            if j in VPATH:
                e(
                    out=t[:].rearrange("p x m -> p (x m)").rearrange("p (b u c) -> p b u c", b=8, u=2),
                    in_=s_raw[j].rearrange("p b k -> p (b k)").bitcast(F32).rearrange("p (b g c u) -> p g b u c", b=8, g=3, u=2)[:, g],
                )
            else:
                e(
                    out=t[:].rearrange("p (a u) m -> p a u m", u=2),
                    in_=s_raw[j][:].rearrange("p a k -> p (a k)").bitcast(F32).rearrange("p (a g m u) -> p g a u m", a=2, g=3, u=2)[:, g],
                )
            s_ord[j, g] = t

        def T(j, g):
            words = s_raw[j][:].rearrange("p a k -> p (a k)").bitcast(F32).rearrange("p (a k) -> p a k", a=2)
            b, t = take()
            for a in range(2):
                for u in range(2):
                    if (j, g) in s_ord:
                        src = s_ord[j, g][:, 2 * a + u, :]
                    else:
                        src = words[:, a, 256 * g + u : 256 * (g + 1) : 2]
                    c0 = P * (2 * a + u)
                    nc.tensor.transpose(t[:, c0 : c0 + P], src, ident[:])
            bank[j, g] = (b, t)

        def V(j, g):
            t = stage.tile([P, 512], F32, name="sturn", tag="sturn", bufs=3, align_bytes=64)
            nc.vector.transpose(out=t[:], in_=s_ord[j, g][:].rearrange("p x c -> p (x c)"))
            grp = stage.tile([P, 256, 4], BF16, name="sgrp", tag="sgrp", bufs=6, align_bytes=64)
            s_grp[j, g] = grp
            bank[j, g] = t

        def Y(j, g, eng="s"):
            e = nc.vector.tensor_copy if eng == "v" else nc.scalar.copy
            e(
                out=s_grp[j, g][:].rearrange("p n k -> p (n k)").bitcast(F32).rearrange("p (b r u) -> p b r u", b=8, u=2),
                in_=bank[j, g][:].rearrange("p (b u r) -> p b r u", b=8, u=2),
            )

        def C(j, g, eng="s"):
            b, t = bank[j, g]
            grp = stage.tile([P, 256, 4], BF16, name="sgrp", tag="sgrp", bufs=6, align_bytes=64)
            e = nc.vector.tensor_copy if eng == "v" else nc.scalar.copy
            e(
                out=grp[:].rearrange("p n k -> p (n k)").bitcast(F32).rearrange("p (a r u) -> p a r u", a=2, u=2),
                in_=t[:].rearrange("p (a u r) -> p a r u", a=2, u=2),
            )
            s_grp[j, g] = grp
            free.append(b)

        def Q(j, g):
            codes = keep.tile([P, 256], U32, name="scode%d_%d" % (j, g), align_bytes=64)
            plane = keep.tile([P, 256], U8, name="splane%d_%d" % (j, g), align_bytes=64)
            nc.vector.quantize_mx(
                out=codes[:].bitcast(E4M3), scales=plane[:], in_=s_grp[j, g][:].rearrange("p n k -> p (n k)")
            )
            s_codes[j, g] = (codes, plane)

        def I(c, h, sc=S_COLS):
            grp = stage.tile([P, NT, 4], BF16, name="wgrp", tag="wgrp", bufs=4, align_bytes=64)
            raw = w_raw[c, h]
            for eng, lo, hi in ((nc.scalar.copy, 0, sc), (nc.vector.tensor_copy, sc, NT)):
                if hi > lo:
                    eng(
                        out=grp[:, lo:hi, :].rearrange("p (c i) t -> p c t i", i=4),
                        in_=raw[:, :, lo:hi].rearrange("p t (c i) -> p c t i", i=4),
                    )
            w_grp[c, h] = grp

        def IG(c, h):
            w_grp[c, h] = stage.tile([P, NT, 4], BF16, name="wgrp", tag="wgrp", bufs=4, align_bytes=64)

        def IX(c, h, e, lo, hi):
            e(
                out=w_grp[c, h][:, lo:hi, :].rearrange("p (c i) t -> p c t i", i=4),
                in_=w_raw[c, h][:, :, lo:hi].rearrange("p t (c i) -> p c t i", i=4),
            )

        def HS(c, h, q, n):
            if (c, h) not in w_grp:
                IG(c, h)
            IX(c, h, nc.scalar.copy, 256 * q, 256 * q + n)

        def HV(c, h, q, n):
            if (c, h) not in w_grp:
                IG(c, h)
            IX(c, h, nc.vector.tensor_copy, 256 * q + n, 256 * q + 256)

        def HW(c, h, q):
            if (c, h) not in w_codes:
                w_codes[c, h] = (
                    keep.tile([P, NT], U32, name="wcode%d_%d" % (c, h), align_bytes=64),
                    keep.tile([P, NT], U8, name="wplane%d_%d" % (c, h), align_bytes=64),
                )
            codes, plane = w_codes[c, h]
            s = slice(256 * q, 256 * q + 256)
            nc.vector.quantize_mx(
                out=codes[:, s].bitcast(E4M3), scales=plane[:, s], in_=w_grp[c, h][:, s, :].rearrange("p w t -> p (w t)")
            )

        def IS(c, h, sc=S_COLS):
            if (c, h) not in w_grp:
                IG(c, h)
            IX(c, h, nc.scalar.copy, 0, sc)

        def IV(c, h, sc=S_COLS):
            if (c, h) not in w_grp:
                IG(c, h)
            IX(c, h, nc.vector.tensor_copy, sc, NT)

        def W(c, h):
            codes = keep.tile([P, NT], U32, name="wcode%d_%d" % (c, h), align_bytes=64)
            plane = keep.tile([P, NT], U8, name="wplane%d_%d" % (c, h), align_bytes=64)
            nc.vector.quantize_mx(
                out=codes[:].bitcast(E4M3), scales=plane[:], in_=w_grp[c, h][:].rearrange("p w t -> p (w t)")
            )
            w_codes[c, h] = (codes, plane)

        acc = {}
        cnt = {}
        outs = {}

        def M(n, c, h):
            if (n, h) not in acc:
                acc[n, h] = take()
                cnt[n, h] = 0
            cnt[n, h] += 1
            t = acc[n, h][1]
            if c < 2:
                cols_n = slice(P * n, P * n + P)
                lhsT, lsc = g_codes[:, c, cols_n].bitcast(E5M2), g_plane[:, c, cols_n]
            else:
                codes, plane = s_codes[n // 2, c - 2]
                cols_n = slice(P * (n % 2), P * (n % 2) + P)
                lhsT, lsc = codes[:, cols_n].bitcast(E4M3), plane[:, cols_n]
            wc, wp = w_codes[c, h]
            nc.tensor.matmul_mx(
                out=t[:], lhsT=lhsT, lhsT_scale=lsc, rhs=wc[:].bitcast(E4M3), rhs_scale=wp[:], start=(cnt[n, h] == 1), stop=(cnt[n, h] == 5)
            )

        def E(n, h):
            b, t = acc[n, h]
            o = stage.tile([P, NT], F32, name="o", tag="o", bufs=OUT_BUFS)
            nc.vector.scalar_tensor_tensor(
                out=o[:], in0=t[:], scalar=cols[:, n : n + 1], in1=theta_b[:, NT * h : NT * h + NT], op0=MULT, op1=ADD
            )
            free.append(b)
            outs[n, h] = o

        def EH(n, h):
            b, t = acc[n, h]
            for q in range(2):
                lo = 256 * q
                o = stage.tile([P, 256], F32, name="oh", tag="oh", bufs=2)
                nc.vector.scalar_tensor_tensor(
                    out=o[:], in0=t[:, lo : lo + 256], scalar=cols[:, n : n + 1],
                    in1=theta_b[:, NT * h + lo : NT * h + lo + 256], op0=MULT, op1=ADD,
                )
                nc.sync.dma_start(out=out[P * n : P * n + P, NT * h + lo : NT * h + lo + 256], in_=o[:])

        def ST(n, h):
            nc.sync.dma_start(out=out[P * n : P * n + P, NT * h : NT * h + NT], in_=outs[n, h][:])

        L_w(0, 0, 0, 256)
        L_w(0, 0, 256, 512)
        L_g(0, 0, 512)
        load_planes()
        L_s(0)
        L_w(1, 0)
        L_g(1, 0, 512)
        L_w(2, 0)
        L_s(1)
        load_small()
        L_w(3, 0)
        L_w(4, 0)
        L_s(2)
        L_g(0, 512, 1536)
        L_g(1, 512, 1536)
        L_s(3)
        L_w(0, 1)
        L_w(1, 1)
        L_w(2, 1)
        L_w(3, 1)
        L_w(4, 1)
        L_v()
        HS(0, 0, 0, 128)
        HV(0, 0, 0, 128)
        HW(0, 0, 0)
        HS(0, 0, 1, 96)
        HV(0, 0, 1, 96)
        HW(0, 0, 1)
        M(0, 0, 0)
        M(1, 0, 0)
        M(2, 0, 0)
        M(3, 0, 0)
        T(0, 0)
        T(0, 1)
        T(0, 2)
        IS(1, 0, 128)
        IV(1, 0, 128)
        C(0, 0)
        C(0, 1)
        C(0, 2)
        W(1, 0)
        M(0, 1, 0)
        M(1, 1, 0)
        M(2, 1, 0)
        M(3, 1, 0)
        Q(0, 0)
        Q(0, 1)
        IS(2, 0, 128)
        IV(2, 0, 128)
        Q(0, 2)
        W(2, 0)
        M(0, 2, 0)
        M(1, 2, 0)
        KA()
        IS(3, 0, 128)
        IV(3, 0, 128)
        T(1, 0)
        T(1, 1)
        T(1, 2)
        KT()
        W(3, 0)
        C(1, 0)
        C(1, 1)
        C(1, 2)
        Q(1, 0)
        KC()
        IS(4, 0, 128)
        IV(4, 0, 128)
        M(0, 3, 0)
        M(1, 3, 0)
        Q(1, 1)
        W(4, 0)
        Q(1, 2)
        M(2, 2, 0)
        M(3, 2, 0)
        M(2, 3, 0)
        M(3, 3, 0)
        R(2, 0, "s")
        R(2, 1, "s")
        R(2, 2, "s")
        KB(0)
        KD(0)
        KB(1)
        KD(1)
        T(2, 0)
        T(2, 1)
        T(2, 2)
        C(2, 0)
        C(2, 1)
        C(2, 2)
        M(0, 4, 0)
        M(1, 4, 0)
        M(2, 4, 0)
        M(3, 4, 0)
        E(0, 0)
        ST(0, 0)
        Q(2, 0)
        Q(2, 1)
        T(3, 0)
        T(3, 1)
        T(3, 2)
        E(1, 0)
        ST(1, 0)
        Q(2, 2)
        E(2, 0)
        ST(2, 0)
        E(3, 0)
        ST(3, 0)
        C(3, 0)
        IS(0, 1, 384)
        IV(0, 1, 384)
        C(3, 1)
        C(3, 2)
        IS(1, 1, 384)
        IV(1, 1, 384)
        Q(3, 0)
        W(0, 1)
        M(4, 0, 0)
        M(4, 1, 0)
        M(4, 2, 0)
        M(4, 3, 0)
        M(4, 4, 0)
        M(5, 0, 0)
        M(5, 1, 0)
        M(5, 2, 0)
        M(5, 3, 0)
        M(5, 4, 0)
        Q(3, 1)
        Q(3, 2)
        E(4, 0)
        ST(4, 0)
        E(5, 0)
        ST(5, 0)
        IS(2, 1, 384)
        IV(2, 1, 384)
        M(6, 0, 0)
        M(6, 1, 0)
        M(6, 2, 0)
        M(6, 3, 0)
        M(6, 4, 0)
        M(7, 0, 0)
        M(7, 1, 0)
        M(7, 2, 0)
        M(7, 3, 0)
        M(7, 4, 0)
        W(1, 1)
        E(6, 0)
        ST(6, 0)
        IS(3, 1, 384)
        IV(3, 1, 384)
        E(7, 0)
        ST(7, 0)
        W(2, 1)
        IS(4, 1, 384)
        IV(4, 1, 384)
        W(3, 1)
        W(4, 1)
        M(0, 0, 1)
        M(1, 0, 1)
        M(2, 0, 1)
        M(3, 0, 1)
        M(4, 0, 1)
        M(5, 0, 1)
        M(6, 0, 1)
        M(7, 0, 1)
        M(0, 1, 1)
        M(1, 1, 1)
        M(2, 1, 1)
        M(3, 1, 1)
        M(4, 1, 1)
        M(5, 1, 1)
        M(6, 1, 1)
        M(7, 1, 1)
        M(0, 2, 1)
        M(1, 2, 1)
        M(2, 2, 1)
        M(3, 2, 1)
        M(4, 2, 1)
        M(5, 2, 1)
        M(6, 2, 1)
        M(7, 2, 1)
        M(0, 3, 1)
        M(1, 3, 1)
        M(2, 3, 1)
        M(3, 3, 1)
        M(4, 3, 1)
        M(5, 3, 1)
        M(6, 3, 1)
        M(7, 3, 1)
        R(4, 0, "s")
        R(4, 1, "s")
        R(4, 2, "s")
        V(4, 0)
        V(4, 1)
        V(4, 2)
        Y(4, 0, "s")
        Y(4, 1, "s")
        Y(4, 2, "s")
        R(5, 0, "s")
        R(5, 1, "s")
        R(5, 2, "s")
        Q(4, 0)
        Q(4, 1)
        Q(4, 2)
        M(0, 4, 1)
        E(0, 1)
        ST(0, 1)
        M(1, 4, 1)
        E(1, 1)
        ST(1, 1)
        M(2, 4, 1)
        E(2, 1)
        ST(2, 1)
        M(3, 4, 1)
        E(3, 1)
        ST(3, 1)
        V(5, 0)
        Y(5, 0, "s")
        M(4, 4, 1)
        E(4, 1)
        ST(4, 1)
        V(5, 1)
        Y(5, 1, "s")
        M(5, 4, 1)
        E(5, 1)
        ST(5, 1)
        V(5, 2)
        Y(5, 2, "s")
        Q(5, 0)
        M(6, 4, 1)
        E(6, 1)
        ST(6, 1)
        Q(5, 1)
        M(7, 4, 1)
        E(7, 1)
        ST(7, 1)
        Q(5, 2)
        M(8, 0, 0)
        M(8, 1, 0)
        M(8, 2, 0)
        M(8, 3, 0)
        M(8, 4, 0)
        E(8, 0)
        ST(8, 0)
        M(8, 0, 1)
        M(8, 1, 1)
        M(8, 2, 1)
        M(8, 3, 1)
        M(8, 4, 1)
        E(8, 1)
        ST(8, 1)
        M(9, 0, 0)
        M(9, 1, 0)
        M(9, 2, 0)
        M(9, 3, 0)
        M(9, 4, 0)
        E(9, 0)
        ST(9, 0)
        M(9, 0, 1)
        M(9, 1, 1)
        M(9, 2, 1)
        M(9, 3, 1)
        M(9, 4, 1)
        E(9, 1)
        ST(9, 1)
        M(10, 0, 0)
        M(10, 1, 0)
        M(10, 2, 0)
        M(10, 3, 0)
        M(10, 4, 0)
        E(10, 0)
        ST(10, 0)
        M(10, 0, 1)
        M(10, 1, 1)
        M(10, 2, 1)
        M(10, 3, 1)
        M(10, 4, 1)
        E(10, 1)
        ST(10, 1)
        M(11, 0, 0)
        M(11, 1, 0)
        M(11, 2, 0)
        M(11, 3, 0)
        M(11, 4, 0)
        E(11, 0)
        ST(11, 0)
        M(11, 0, 1)
        M(11, 1, 1)
        M(11, 2, 1)
        M(11, 3, 1)
        M(11, 4, 1)
        EH(11, 1)


OUT_BUFS = 12
